import numpy as np, ml_dtypes
CORES = [0,1,2,3,4,5,6,7]
N = 8
PERM = [[0,3],[1,4],[2,5],[3,6],[4,7],[5,0],[6,1],[7,2]]
def setup_inputs(rng):
    return {"x": rng.standard_normal((N, 128, 2048), dtype=np.float32).astype(ml_dtypes.bfloat16)}
def reference(x):
    y = np.empty_like(x)
    for s, d in PERM:
        y[d] = x[s]
    return {"y": y}

K = 4
COLS = 2048
W = COLS // K

SCRATCH = {
    "stage": ("sbuf", [128, COLS], "bfloat16"),
    "land": ("sbuf", [128, COLS], "bfloat16"),
}
SEMAPHORES = ["ld%d" % k for k in range(K)] + ["ar%d" % k for k in range(K)] + ["sent", "stored"]


def rank_program(g, core, T, topo):
    rank = T.rank_of(core)
    if rank is None:
        return
    perm = T.tables["PERM"]
    dst = [d for s, d in perm if s == rank]
    src = [s for s, d in perm if d == rank]
    to_self = bool(dst) and dst[0] == rank
    blocks = [slice(k * W, (k + 1) * W) for k in range(K)]

    if dst:
        for k, b in enumerate(blocks):
            g.sync.dma_start(T.stage[:, b], T.x[:, b]).then_inc(T.sem["ld%d" % k], 16)

    if to_self:
        for k, b in enumerate(blocks):
            g.scalar.wait_ge(T.sem["ld%d" % k], 16)
            g.scalar.dma_start(T.y[:, b], T.stage[:, b]).then_inc(T.sem.stored, 16)
        g.scalar.wait_ge(T.sem.stored, 16 * K)
        return

    if dst:
        dcore = T.cores[dst[0]]
        rid, pid, _se = topo.addr(dcore)
        mask = topo.mask(core, dcore)
        for k, b in enumerate(blocks):
            g.wait_ge(T.sem["ld%d" % k], 16)
            g.remote_dma(T.land[:, b], T.stage[:, b], T.sem["ar%d" % k], T.sem.sent, pid, rid, mask)

    if src:
        for k, b in enumerate(blocks):
            g.scalar.wait_ge(T.sem["ar%d" % k], 16)
            g.scalar.dma_start(T.y[:, b], T.land[:, b]).then_inc(T.sem.stored, 16)
        g.scalar.wait_ge(T.sem.stored, 16 * K)

    if dst:
        g.wait_ge(T.sem.sent, 16 * K)
